import numpy as np
import ml_dtypes


def mxq(x, axis, fmt="e4m3"):
    dtype, down = {"e4m3": (ml_dtypes.float8_e4m3fn, 7), "e5m2": (ml_dtypes.float8_e5m2, 14)}[fmt]
    v = np.moveaxis(np.asarray(x, np.float32).astype(ml_dtypes.bfloat16).astype(np.float64), axis, -1)
    blocks = v.reshape(v.shape[:-1] + (-1, 32))
    amax = np.abs(blocks).max(-1, keepdims=True)
    byte = np.maximum(np.where(amax > 0, np.frexp(amax)[1] - 1 + 127, 0) - down, 1)
    scale = np.exp2(byte - 127.0)
    codes = (blocks / scale).astype(np.float32).astype(dtype).astype(np.float64)
    return np.moveaxis((codes * scale).reshape(v.shape), -1, axis)


WIDE = False


def mx_kscale(k):
    if not WIDE:
        return np.ones(k)
    levels = np.array([10, -10, 5, -5, 0])
    if k % 512:
        return np.exp2(np.random.permutation(np.resize(levels, k // 32))).repeat(32)
    a = np.empty((k // 512, 16))
    for p in range(k // 512):
        a[p, :8] = np.random.permutation(np.resize(levels, 8))
        for g in range(8):
            far = levels[np.abs(levels - a[p, g]) >= 10]
            a[p, g + 8] = far[np.random.randint(len(far))]
    return np.exp2(a.ravel()).repeat(32)


BF16 = ml_dtypes.bfloat16


def bf(x):
    return np.asarray(x, np.float32).astype(BF16)


def f64(x):
    return np.asarray(x).astype(np.float64)


E2M1 = np.array([0.0, 0.5, 1.0, 1.5, 2.0, 3.0, 4.0, 6.0, -0.0, -0.5, -1.0, -1.5, -2.0, -3.0, -4.0, -6.0])


def pack_weight(w, fmt):
    k, n = w.shape
    w = f64(bf(w)).reshape(k // 32, 32, n)
    amax = np.abs(w).max(1)
    if fmt == "e4m3":
        byte = np.frexp(amax)[1] - 1 + 127 - 7
    else:
        mant, ex = np.frexp(amax / 6.0)
        byte = np.where(mant > 0.5, ex, ex - 1) + 127
    byte = np.clip(np.where(amax > 0, byte, 1), 1, 254)
    scaled = (w * np.exp2(127.0 - byte)[:, None, :]).reshape(k, n).astype(np.float32)
    by_word = np.ascontiguousarray(scaled.reshape(k // 512, 128, 4, n).transpose(0, 1, 3, 2))
    if fmt == "e4m3":
        words = by_word.astype(ml_dtypes.float8_e4m3fn).view(np.uint8)
    else:
        c = by_word.astype(ml_dtypes.float4_e2m1fn).view(np.uint8) & 0xF
        words = c[..., 0::2] | (c[..., 1::2] << 4)
    return np.ascontiguousarray(words), np.ascontiguousarray(byte.astype(np.uint8).reshape(k // 512, 16, n))


def unpack_weight(words, scales, fmt):
    g, p, n, _ = words.shape
    if fmt == "e4m3":
        vals = np.ascontiguousarray(words).view(ml_dtypes.float8_e4m3fn).astype(np.float64)
    else:
        nib = np.empty((g, p, n, 4), np.uint8)
        nib[..., 0::2] = words & 0xF
        nib[..., 1::2] = words >> 4
        vals = E2M1[nib]
    vals = vals * np.repeat(np.exp2(scales.astype(np.float64) - 127.0), 8, axis=1)[..., None]
    return vals.transpose(0, 1, 3, 2).reshape(g * 512, n)
def pack4(w):
    words, scales = pack_weight(w, "e2m1")
    return words.reshape(words.shape[0], 128, -1), scales


def unpack4(words, scales):
    return unpack_weight(words.reshape(words.shape[0], 128, -1, 2), scales, "e2m1")


E4M3FN = np.array([(-1.0 if i & 128 else 1.0) * ((1.0 + (i & 7) / 8.0) * 2.0 ** (((i >> 3) & 15) - 7) if i & 120 else (i & 7) * 2.0 ** -9) for i in range(256)])


def e4m3fn_bytes(y):
    return np.clip(np.asarray(y, np.float64), -448.0, 448.0).astype(np.float32).astype(ml_dtypes.float8_e4m3fn).view(np.uint8)


def e4m3fn_values(b):
    return E4M3FN[b]


P, N, D, K = 2, 512, 1024, 512


def softplus(v):
    return np.maximum(v, 0.0) + np.log(1.0 + np.exp(-np.abs(v)))


def draw0():
    s, t = mx_kscale(D), mx_kscale(K)
    h = bf(np.random.standard_normal((P, N, D)) * s)
    wa_words, wa_scales = pack4(np.random.standard_normal((D, K)) / np.sqrt(D) / s[:, None] * t)
    wb_words, wb_scales = pack4(np.random.standard_normal((D, K)) / np.sqrt(D) / s[:, None] / t)
    return {"h": h,
            "wa_words": wa_words, "wa_scales": wa_scales,
            "wb_words": wb_words, "wb_scales": wb_scales,
            "gate": bf(np.random.standard_normal((P, K)))}


def core(h, wa_words, wa_scales, wb_words, wb_scales, gate):
    hq = mxq(f64(h), 2, "e4m3")
    a = hq @ unpack4(wa_words, wa_scales)
    b = hq @ unpack4(wb_words, wb_scales)
    lam = softplus(f64(gate))
    al = a * lam[:, None, :]
    x = mxq(al, 2, "e4m3") @ mxq(b, 2, "e4m3").transpose(0, 2, 1)
    s = (x - np.swapaxes(x, 1, 2)) / np.sqrt(K)
    return -softplus(-s)


def setup_inputs():
    drawn = draw0()
    full = np.asarray(drawn['h']).astype(np.float64)
    scale = (np.abs(full).reshape(2, 4, 128, 8, 128).max(axis=(2, 4)) / 448.0).astype(np.float32)
    given = {}
    for key, value in drawn.items():
        if key == 'h':
            given['h_bytes'] = e4m3fn_bytes(full / np.repeat(np.repeat(scale.astype(np.float64), 128, axis=1), 128, axis=2))
            given['h_scale'] = scale
        else:
            given[key] = value
    return given


def reference(h_bytes, h_scale, wa_words, wa_scales, wb_words, wb_scales, gate):
    return core(e4m3fn_values(h_bytes) * np.repeat(np.repeat(h_scale.astype(np.float64), 128, axis=1), 128, axis=2), wa_words, wa_scales, wb_words, wb_scales, gate)

@@ -1,0 +1,299 @@
+from contextlib import ExitStack
+
+import concourse.mybir as mybir
+from concourse.masks import make_identity
+
+NP, N, D, K = 2, 512, 1024, 512
+P = 128
+NT = N // P
+G = D // 512
+FLOPS = 2 * NP * (2 * N * D * K + N * N * K)
+C = K ** -0.5
+TINY = 2.0 ** -60
+
+F32 = mybir.dt.float32
+BF16 = mybir.dt.bfloat16
+I32 = mybir.dt.int32
+U32 = mybir.dt.uint32
+U8 = mybir.dt.uint8
+FP8 = mybir.dt.float8_e4m3fn
+FP8X4 = mybir.dt.float8_e4m3fn_x4
+FP4X4 = mybir.dt.float4_e2m1fn_x4
+ALU = mybir.AluOpType
+ACT = mybir.ActivationFunctionType
+
+
+def tile_generalpreferenceskewembeddingscores_d2p_kernel(
+    tc, h_bytes, h_scale, wa_words, wa_scales, wb_words, wb_scales, gate, out
+):
+    nc = tc.nc
+    with ExitStack() as ctx:
+        sb = ctx.enter_context(tc.tile_pool(name="sb", bufs=1))
+        ps = ctx.enter_context(tc.psum_pool(name="ps", bufs=1))
+        ctx.enter_context(tc.manual_schedule())
+
+        def bank(tag, shape, name):
+            return ps.tile(shape, F32, name=name, tag=tag, bufs=(4 if tag == "x" else 2))
+
+        gate_rows = sb.tile([P, P], BF16, name="gate_rows")
+        gate_f32 = sb.tile([P, P], F32, name="gate_f32")
+        ident = sb.tile([P, P], F32, name="ident")
+        w_raw = [sb.tile([P, G, 1024], U8, name=f"w_raw{w}", align_bytes=64) for w in range(2)]
+        w_perm = [sb.tile([P, G, 4, 256], U8, name=f"w_perm{w}", align_bytes=64) for w in range(2)]
+        s_raw = [sb.tile([P, G, K], U8, name=f"s_raw{w}", align_bytes=64) for w in range(2)]
+        s_perm = [sb.tile([P, G, 4, P], U8, name=f"s_perm{w}", align_bytes=64) for w in range(2)]
+        scales = sb.tile([P, NP * NT * 8], F32, name="scales")
+        tiny = sb.tile([P, 1], F32, name="tiny")
+        warm = sb.tile([P, 1], F32, name="warm")
+
+        nc.gpsimd.memset(gate_rows[:], 0.0)
+        for w in range(2):
+            nc.gpsimd.memset(s_raw[w][:].rearrange("p g k -> p (g k)").bitcast(I32), 0)
+        make_identity(nc, ident[:])
+        nc.vector.memset(tiny[:], TINY)
+        nc.vector.memset(warm[:], 0.0)
+
+        nc.scalar.dma_start(
+            out=scales[:], in_=h_scale.rearrange("a i j -> (a i j)").partition_broadcast(P)
+        )
+        gv = gate.rearrange("a (q t r) -> a t q r", q=16, t=4, r=8)
+        for a in range(NP):
+            nc.scalar.dma_start(
+                out=gate_rows[4 * a : 4 * a + 4, :].rearrange("t (q r) -> t q r", q=16), in_=gv[a]
+            )
+        nc.scalar.activation(out=warm[:], in_=warm[:], func=ACT.Exp)
+
+        codes_in = {}
+
+        def load_h(a, first, count):
+            t = sb.tile([P, count, D], U8, name=f"h_bytes{a}_{first}", align_bytes=64)
+            nc.sync.dma_start(
+                out=t[:],
+                in_=h_bytes[a, first * P : (first + count) * P, :].rearrange("(i p) k -> p i k", p=P),
+            )
+            for i in range(count):
+                codes_in[a * NT + first + i] = (t, i)
+
+        def load_words(w, words):
+            nc.sync.dma_start(
+                out=w_raw[w][:].rearrange("p g b -> p (g b)").bitcast(I32).rearrange("p (g c) -> p g c", g=G),
+                in_=words.bitcast(I32).rearrange("g p c -> p g c"),
+            )
+
+        def load_scales(w, src):
+            v = src.bitcast(I32).rearrange("g (q r) c -> q r g c", r=4)
+            d = s_raw[w][:].rearrange("p g k -> p (g k)").bitcast(I32).rearrange("p (g c) -> p g c", g=G)
+            for q in range(4):
+                nc.sync.dma_start(out=d[32 * q : 32 * q + 4], in_=v[q])
+
+        load_h(0, 0, 1)
+        load_h(0, 1, 1)
+        load_words(0, wa_words)
+        load_scales(0, wa_scales)
+        load_h(0, 2, 1)
+        load_words(1, wb_words)
+        load_scales(1, wb_scales)
+        load_h(0, 3, 1)
+        load_h(1, 0, 2)
+        load_h(1, 2, 2)
+
+        nc.gpsimd.tensor_copy(out=gate_f32[:], in_=gate_rows[:])
+
+        wide, pt, hg, hc, hs = {}, {}, {}, {}, {}
+        pa, pb, ab, nal = {}, {}, {}, {}
+        kc = [sb.tile([P, 3, N], U32, name=f"kc{a}", align_bytes=64) for a in range(NP)]
+        ks = [sb.tile([P, 3, N], U8, name=f"ks{a}", align_bytes=64) for a in range(NP)]
+        px, sig, logs = {}, {}, {}
+        lam = sb.tile([P, NP * 4], F32, name="lam")
+        g_sb = sb.tile([P, NP * 4], F32, name="g_sb")
+        g_abs = sb.tile([P, NP * 4], F32, name="g_abs")
+        g_exp = sb.tile([P, NP * 4], F32, name="g_exp")
+        g_ln = sb.tile([P, NP * 4], F32, name="g_ln")
+
+        def gate_turn():
+            pg = bank("x", [P, P], "pg")
+            nc.tensor.transpose(pg[:], gate_f32[:], ident[:])
+            nc.scalar.copy(out=g_sb[:], in_=pg[:, 0 : NP * 4])
+            nc.scalar.activation(out=g_abs[:], in_=g_sb[:], func=ACT.Abs)
+            nc.scalar.activation(out=g_exp[:], in_=g_abs[:], func=ACT.Exp, scale=-1.0)
+
+        def gate_ln():
+            nc.scalar.activation(out=g_ln[:], in_=g_exp[:], func=ACT.Ln, bias=1.0)
+
+        def gate_lam():
+            nc.vector.scalar_tensor_tensor(
+                out=lam[:], in0=g_sb[:], scalar=0.0, in1=g_ln[:], op0=ALU.max, op1=ALU.add
+            )
+
+        def W(T):
+            t, i = codes_in[T]
+            wide[T] = sb.tile([P, D], BF16, name=f"wide{T}", align_bytes=64)
+            for j in range(8):
+                nc.vector.tensor_scalar(
+                    out=wide[T][:, P * j : P * (j + 1)],
+                    in0=t[:, i, P * j : P * (j + 1)].bitcast(FP8),
+                    scalar1=scales[:, 8 * T + j : 8 * T + j + 1],
+                    scalar2=None,
+                    op0=ALU.mult,
+                )
+
+        def X(T):
+            pt[T] = bank("t", [P, 2 * G, P], f"pt{T}")
+            words = wide[T][:].bitcast(F32)
+            for g in range(G):
+                for u in range(2):
+                    nc.tensor.transpose(
+                        pt[T][:, 2 * g + u, :], words[:, 256 * g + u : 256 * (g + 1) : 2], ident[:]
+                    )
+
+        def E(T):
+            hg[T] = sb.tile([P, G * P * 4], BF16, name=f"hg{T}", align_bytes=64)
+            nc.scalar.copy(
+                out=hg[T][:].bitcast(F32).rearrange("p (g n u) -> p g n u", g=G, u=2),
+                in_=pt[T][:].rearrange("p (g u) n -> p g n u", g=G),
+            )
+
+        def Q(T):
+            hc[T] = sb.tile([P, G * P], U32, name=f"hc{T}", align_bytes=64)
+            hs[T] = sb.tile([P, G * P], U8, name=f"hs{T}", align_bytes=64)
+            nc.vector.quantize_mx(out=hc[T][:].bitcast(FP8X4), scales=hs[T][:], in_=hg[T][:])
+
+        def PERM(w):
+            for g in range(G):
+                nc.vector.tensor_copy(
+                    out=w_perm[w][:, g].rearrange("p t b -> p (t b)").bitcast(I32).rearrange("p (t q x) -> p q t x", t=4, x=4),
+                    in_=w_raw[w][:, g].bitcast(I32).rearrange("p (q t x) -> p q t x", t=4, x=4),
+                )
+            for g in range(G):
+                nc.vector.tensor_copy(
+                    out=s_perm[w][:, g].rearrange("p t b -> p (t b)").bitcast(I32).rearrange("p (t q x) -> p q t x", t=4, x=2),
+                    in_=s_raw[w][:, g].bitcast(I32).rearrange("p (q t x) -> p q t x", t=4, x=2),
+                )
+
+        def M(T):
+            for w, store in ((0, pa), (1, pb)):
+                store[T] = bank("ab", [P, 4, P], f"p{w}_{T}")
+                for t in range(4):
+                    for g in range(G):
+                        nc.tensor.matmul_mx(
+                            out=store[T][:, t, :],
+                            lhsT=w_perm[w][:, g, t, :].bitcast(FP4X4),
+                            lhsT_scale=s_perm[w][:, g, t, :],
+                            rhs=hc[T][:, P * g : P * (g + 1)].bitcast(FP8X4),
+                            rhs_scale=hs[T][:, P * g : P * (g + 1)],
+                            start=(g == 0),
+                            stop=(g == G - 1),
+                        )
+
+        def pair_tile(T):
+            r = T // 2
+            if r not in ab:
+                ab[r] = sb.tile([P, 2, 2, 512], BF16, name=f"ab{r}", align_bytes=64)
+            return ab[r]
+
+        def A(T):
+            a = T // NT
+            nc.vector.tensor_tensor(
+                out=pair_tile(T)[:, 0, T % 2, :].rearrange("p (n t) -> p n t", t=4),
+                in0=pa[T][:].rearrange("p t n -> p n t"),
+                in1=lam[:, 4 * a : 4 * a + 4].unsqueeze(1).to_broadcast([P, P, 4]),
+                op=ALU.mult,
+            )
+
+        def B(T):
+            nc.scalar.copy(
+                out=pair_tile(T)[:, 1, T % 2, :].rearrange("p (n t) -> p n t", t=4),
+                in_=pb[T][:].rearrange("p t n -> p n t"),
+            )
+
+        def NR(r):
+            a, cols = r // 2, slice(256 * (r % 2), 256 * (r % 2) + 256)
+            nal[r] = sb.tile([P, 1024], BF16, name=f"nal{r}", align_bytes=64)
+            al = ab[r][:, 0].rearrange("p i n -> p (i n)")
+            b = ab[r][:, 1].rearrange("p i n -> p (i n)")
+            nc.vector.tensor_scalar(out=nal[r][:], in0=al, scalar1=-1.0, scalar2=None, op0=ALU.mult)
+            for k, src in ((1, b), (0, al), (2, nal[r][:])):
+                nc.vector.quantize_mx(out=kc[a][:, k, cols].bitcast(FP8X4), scales=ks[a][:, k, cols], in_=src)
+
+        def XX(a, n):
+            tag = "x" if a == 0 else ("t" if n < 2 else "ab")
+            x = px[a, n] = bank(tag, [P, N], f"px{a}_{n}")
+            rows = slice(P * n, P * (n + 1))
+            for s, m in ((0, 1), (1, 2)):
+                nc.tensor.matmul_mx(
+                    out=x[:],
+                    lhsT=kc[a][:, s, rows].bitcast(FP8X4),
+                    lhsT_scale=ks[a][:, s, rows],
+                    rhs=kc[a][:, m, :].bitcast(FP8X4),
+                    rhs_scale=ks[a][:, m, :],
+                    start=(s == 0),
+                    stop=(s == 1),
+                )
+            sig[a, n] = sb.tile([P, N], F32, name=f"sig{a}_{n}")
+            nc.scalar.activation(out=sig[a, n][:], in_=x[:], func=ACT.Sigmoid, scale=C)
+
+        def LF(a, n):
+            logs[a, n] = sb.tile([P, N], F32, name=f"logs{a}_{n}")
+            nc.scalar.activation(out=logs[a, n][:], in_=sig[a, n][:], func=ACT.Ln, bias=tiny[:])
+            o = sb.tile([P, N], F32, name=f"o{a}_{n}")
+            nc.vector.scalar_tensor_tensor(
+                out=o[:], in0=px[a, n][:], scalar=C, in1=logs[a, n][:], op0=ALU.mult, op1=ALU.min
+            )
+            nc.sync.dma_start(out=out[a, P * n : P * (n + 1), :], in_=o[:])
+
+        gate_turn()
+        W(0); X(0); E(0)
+        W(1); X(1); E(1)
+        gate_ln()
+        PERM(0)
+        W(2); X(2); E(2)
+        Q(0)
+        PERM(1)
+        M(0)
+        Q(1)
+        B(0)
+        W(3); X(3); E(3)
+        gate_lam()
+        A(0)
+        M(1)
+        Q(2)
+        B(1); A(1)
+        M(2)
+        Q(3)
+        B(2)
+        W(4); X(4); E(4)
+        NR(0)
+        A(2)
+        M(3)
+        B(3)
+        W(5); X(5); E(5)
+        Q(4)
+        A(3)
+        M(4)
+        B(4)
+        W(6); X(6); E(6)
+        NR(1)
+        XX(0, 0)
+        XX(0, 1)
+        Q(5)
+        A(4)
+        M(5)
+        B(5)
+        W(7); X(7); E(7)
+        XX(0, 2)
+        XX(0, 3)
+        Q(6)
+        A(5)
+        M(6)
+        B(6)
+        NR(2)
+        Q(7)
+        A(6)
+        M(7)
+        B(7); A(7)
+        NR(3)
+        for n in range(NT):
+            XX(1, n)
+        for a in range(NP):
+            for n in range(NT):
+                LF(a, n)

@@ -35,9 +35,9 @@ def tile_generalpreferenceskewembeddingscores_d2p_kernel(
         def bank(tag, shape, name):
             return ps.tile(shape, F32, name=name, tag=tag, bufs=(4 if tag == "x" else 2))
 
-        gate_rows = sb.tile([P, P], BF16, name="gate_rows")
-        gate_f32 = sb.tile([P, P], F32, name="gate_f32")
+        gate_rows = sb.tile([P, NP * P], BF16, name="gate_rows")
         ident = sb.tile([P, P], F32, name="ident")
+        ident16 = sb.tile([P, P], BF16, name="ident16")
         w_raw = [sb.tile([P, G, 1024], U8, name=f"w_raw{w}", align_bytes=64) for w in range(2)]
         w_perm = [sb.tile([P, G, 4, 256], U8, name=f"w_perm{w}", align_bytes=64) for w in range(2)]
         s_raw = [sb.tile([P, G, K], U8, name=f"s_raw{w}", align_bytes=64) for w in range(2)]
@@ -46,21 +46,21 @@ def tile_generalpreferenceskewembeddingscores_d2p_kernel(
         tiny = sb.tile([P, 1], F32, name="tiny")
         warm = sb.tile([P, 1], F32, name="warm")
 
-        nc.gpsimd.memset(gate_rows[:], 0.0)
-        for w in range(2):
-            nc.gpsimd.memset(s_raw[w][:].rearrange("p g k -> p (g k)").bitcast(I32), 0)
-        make_identity(nc, ident[:])
-        nc.vector.memset(tiny[:], TINY)
+        nc.vector.memset(gate_rows[:], 0.0)
         nc.vector.memset(warm[:], 0.0)
+        for w in range(2):
+            nc.vector.memset(s_raw[w][:].rearrange("p g k -> p (g k)").bitcast(I32), 0)
+        nc.vector.memset(tiny[:], TINY)
+        make_identity(nc, ident16[:])
+        make_identity(nc, ident[:])
 
+        nc.scalar.dma_start(
+            out=gate_rows[0:4, :].rearrange("t (q r) -> t q r", r=8),
+            in_=gate.rearrange("a (q t r) -> t (a q) r", t=4, r=8),
+        )
         nc.scalar.dma_start(
             out=scales[:], in_=h_scale.rearrange("a i j -> (a i j)").partition_broadcast(P)
         )
-        gv = gate.rearrange("a (q t r) -> a t q r", q=16, t=4, r=8)
-        for a in range(NP):
-            nc.scalar.dma_start(
-                out=gate_rows[4 * a : 4 * a + 4, :].rearrange("t (q r) -> t q r", q=16), in_=gv[a]
-            )
         nc.scalar.activation(out=warm[:], in_=warm[:], func=ACT.Exp)
 
         codes_in = {}
@@ -89,32 +89,30 @@ def tile_generalpreferenceskewembeddingscores_d2p_kernel(
         load_h(0, 0, 1)
         load_h(0, 1, 1)
         load_words(0, wa_words)
+        load_h(0, 2, 2)
         load_scales(0, wa_scales)
-        load_h(0, 2, 1)
         load_words(1, wb_words)
         load_scales(1, wb_scales)
-        load_h(0, 3, 1)
         load_h(1, 0, 2)
         load_h(1, 2, 2)
-
-        nc.gpsimd.tensor_copy(out=gate_f32[:], in_=gate_rows[:])
 
         wide, pt, hg, hc, hs = {}, {}, {}, {}, {}
         pa, pb, ab, nal = {}, {}, {}, {}
         kc = [sb.tile([P, 3, N], U32, name=f"kc{a}", align_bytes=64) for a in range(NP)]
         ks = [sb.tile([P, 3, N], U8, name=f"ks{a}", align_bytes=64) for a in range(NP)]
         px, sig, logs = {}, {}, {}
-        lam = sb.tile([P, NP * 4], F32, name="lam")
-        g_sb = sb.tile([P, NP * 4], F32, name="g_sb")
-        g_abs = sb.tile([P, NP * 4], F32, name="g_abs")
-        g_exp = sb.tile([P, NP * 4], F32, name="g_exp")
-        g_ln = sb.tile([P, NP * 4], F32, name="g_ln")
+        lam = sb.tile([P, NP, 4], F32, name="lam")
+        g_sb = sb.tile([P, NP, 4], F32, name="g_sb")
+        g_abs = sb.tile([P, NP, 4], F32, name="g_abs")
+        g_exp = sb.tile([P, NP, 4], F32, name="g_exp")
+        g_ln = sb.tile([P, NP, 4], F32, name="g_ln")
 
         def gate_turn():
-            pg = bank("x", [P, P], "pg")
-            nc.tensor.transpose(pg[:], gate_f32[:], ident[:])
-            nc.scalar.copy(out=g_sb[:], in_=pg[:, 0 : NP * 4])
-            nc.scalar.activation(out=g_abs[:], in_=g_sb[:], func=ACT.Abs)
+            pg = ps.tile([P, NP, P], BF16, name="pg", tag="x", bufs=4)
+            for a in range(NP):
+                nc.tensor.transpose(pg[:, a, :], gate_rows[:, P * a : P * (a + 1)], ident16[:])
+            nc.scalar.activation(out=g_abs[:], in_=pg[:, :, 0:4], func=ACT.Abs)
+            nc.scalar.copy(out=g_sb[:], in_=pg[:, :, 0:4])
             nc.scalar.activation(out=g_exp[:], in_=g_abs[:], func=ACT.Exp, scale=-1.0)
 
         def gate_ln():
@@ -172,7 +170,7 @@ def tile_generalpreferenceskewembeddingscores_d2p_kernel(
 
         def M(T):
             for w, store in ((0, pa), (1, pb)):
-                store[T] = bank("ab", [P, 4, P], f"p{w}_{T}")
+                store[T] = bank("x" if T in (1, 3) else "ab", [P, 4, P], f"p{w}_{T}")
                 for t in range(4):
                     for g in range(G):
                         nc.tensor.matmul_mx(
@@ -196,7 +194,7 @@ def tile_generalpreferenceskewembeddingscores_d2p_kernel(
             nc.vector.tensor_tensor(
                 out=pair_tile(T)[:, 0, T % 2, :].rearrange("p (n t) -> p n t", t=4),
                 in0=pa[T][:].rearrange("p t n -> p n t"),
-                in1=lam[:, 4 * a : 4 * a + 4].unsqueeze(1).to_broadcast([P, P, 4]),
+                in1=lam[:, a : a + 1, :].to_broadcast([P, P, 4]),
                 op=ALU.mult,
             )
 
@@ -241,57 +239,35 @@ def tile_generalpreferenceskewembeddingscores_d2p_kernel(
             )
             nc.sync.dma_start(out=out[a, P * n : P * (n + 1), :], in_=o[:])
 
+        T_ALL = NP * NT
         gate_turn()
-        W(0); X(0); E(0)
-        W(1); X(1); E(1)
-        gate_ln()
-        PERM(0)
-        W(2); X(2); E(2)
-        Q(0)
-        PERM(1)
-        M(0)
-        Q(1)
-        B(0)
-        W(3); X(3); E(3)
-        gate_lam()
-        A(0)
-        M(1)
-        Q(2)
-        B(1); A(1)
-        M(2)
-        Q(3)
-        B(2)
-        W(4); X(4); E(4)
-        NR(0)
-        A(2)
-        M(3)
-        B(3)
-        W(5); X(5); E(5)
-        Q(4)
-        A(3)
-        M(4)
-        B(4)
-        W(6); X(6); E(6)
-        NR(1)
-        XX(0, 0)
-        XX(0, 1)
-        Q(5)
-        A(4)
-        M(5)
-        B(5)
-        W(7); X(7); E(7)
-        XX(0, 2)
-        XX(0, 3)
-        Q(6)
-        A(5)
-        M(6)
-        B(6)
-        NR(2)
-        Q(7)
-        A(6)
-        M(7)
-        B(7); A(7)
-        NR(3)
+        for k in range(-4, T_ALL + 2):
+            if k == -4:
+                gate_ln()
+            if 0 <= k + 2 < T_ALL:
+                E(k + 2)
+            if k + 4 < T_ALL:
+                W(k + 4)
+            if k == -3:
+                PERM(0)
+            if k == -2:
+                PERM(1)
+            if k == -1:
+                gate_lam()
+            if k + 4 < T_ALL:
+                X(k + 4)
+            if 0 <= k + 2 < T_ALL:
+                Q(k + 2)
+            if 0 <= k < T_ALL:
+                A(k)
+                B(k)
+            for T in range(T_ALL):
+                if k == (T - 2 if T < 5 else T - 1):
+                    M(T)
+            if 1 <= k - 1 < T_ALL and (k - 1) % 2 == 1:
+                NR((k - 1) // 2)
+            for n in {6: (0,), 7: (1, 2, 3)}.get(k, ()):
+                XX(0, n)
         for n in range(NT):
             XX(1, n)
         for a in range(NP):

@@ -32,8 +32,8 @@ def tile_generalpreferenceskewembeddingscores_d2p_kernel(
         ps = ctx.enter_context(tc.psum_pool(name="ps", bufs=1))
         ctx.enter_context(tc.manual_schedule())
 
-        def bank(tag, shape, name):
-            return ps.tile(shape, F32, name=name, tag=tag, bufs=(4 if tag == "x" else 2))
+        def bank(b, shape, name, dtype=F32):
+            return ps.tile(shape, dtype, name=name, tag=f"bank{b}")
 
         gate_rows = sb.tile([P, NP * P], BF16, name="gate_rows")
         ident = sb.tile([P, P], F32, name="ident")
@@ -107,12 +107,20 @@ def tile_generalpreferenceskewembeddingscores_d2p_kernel(
         g_exp = sb.tile([P, NP, 4], F32, name="g_exp")
         g_ln = sb.tile([P, NP, 4], F32, name="g_ln")
 
+        ps_gate = {}
+
         def gate_turn():
-            pg = ps.tile([P, NP, P], BF16, name="pg", tag="x", bufs=4)
+            pg = bank(7, [P, NP, P], "pg", BF16)
+            ps_gate["pg"] = pg
             for a in range(NP):
                 nc.tensor.transpose(pg[:, a, :], gate_rows[:, P * a : P * (a + 1)], ident16[:])
+
+        def gate_out():
+            pg = ps_gate["pg"]
             nc.scalar.activation(out=g_abs[:], in_=pg[:, :, 0:4], func=ACT.Abs)
             nc.scalar.copy(out=g_sb[:], in_=pg[:, :, 0:4])
+
+        def gate_exp():
             nc.scalar.activation(out=g_exp[:], in_=g_abs[:], func=ACT.Exp, scale=-1.0)
 
         def gate_ln():
@@ -128,20 +136,22 @@ def tile_generalpreferenceskewembeddingscores_d2p_kernel(
             wide[T] = sb.tile([P, D], BF16, name=f"wide{T}", align_bytes=64)
             for j in range(8):
                 nc.vector.tensor_scalar(
-                    out=wide[T][:, P * j : P * (j + 1)],
-                    in0=t[:, i, P * j : P * (j + 1)].bitcast(FP8),
+                    out=wide[T][:, 512 * (j // 4) : 512 * (j // 4 + 1)].rearrange("p (u w e) -> p w u e", u=2, e=2)[
+                        :, 32 * (j % 4) : 32 * (j % 4 + 1)
+                    ],
+                    in0=t[:, i, P * j : P * (j + 1)].bitcast(FP8).rearrange("p (w u e) -> p w u e", u=2, e=2),
                     scalar1=scales[:, 8 * T + j : 8 * T + j + 1],
                     scalar2=None,
                     op0=ALU.mult,
                 )
 
         def X(T):
-            pt[T] = bank("t", [P, 2 * G, P], f"pt{T}")
+            pt[T] = bank(T % 2, [P, 2 * G, P], f"pt{T}")
             words = wide[T][:].bitcast(F32)
             for g in range(G):
                 for u in range(2):
                     nc.tensor.transpose(
-                        pt[T][:, 2 * g + u, :], words[:, 256 * g + u : 256 * (g + 1) : 2], ident[:]
+                        pt[T][:, 2 * g + u, :], words[:, 256 * g + P * u : 256 * g + P * (u + 1)], ident[:]
                     )
 
         def E(T):
@@ -168,9 +178,9 @@ def tile_generalpreferenceskewembeddingscores_d2p_kernel(
                     in_=s_raw[w][:, g].bitcast(I32).rearrange("p (q t x) -> p q t x", t=4, x=2),
                 )
 
-        def M(T):
-            for w, store in ((0, pa), (1, pb)):
-                store[T] = bank("x" if T in (1, 3) else "ab", [P, 4, P], f"p{w}_{T}")
+        def M(w, T):
+            for store in ((pa, pb)[w],):
+                store[T] = bank({1: 4, 3: 6}.get(T, 2) + w, [P, 4, P], f"p{w}_{T}")
                 for t in range(4):
                     for g in range(G):
                         nc.tensor.matmul_mx(
@@ -204,18 +214,33 @@ def tile_generalpreferenceskewembeddingscores_d2p_kernel(
                 in_=pb[T][:].rearrange("p t n -> p n t"),
             )
 
-        def NR(r):
-            a, cols = r // 2, slice(256 * (r % 2), 256 * (r % 2) + 256)
-            nal[r] = sb.tile([P, 1024], BF16, name=f"nal{r}", align_bytes=64)
-            al = ab[r][:, 0].rearrange("p i n -> p (i n)")
-            b = ab[r][:, 1].rearrange("p i n -> p (i n)")
-            nc.vector.tensor_scalar(out=nal[r][:], in0=al, scalar1=-1.0, scalar2=None, op0=ALU.mult)
-            for k, src in ((1, b), (0, al), (2, nal[r][:])):
-                nc.vector.quantize_mx(out=kc[a][:, k, cols].bitcast(FP8X4), scales=ks[a][:, k, cols], in_=src)
+        GROUPS = ((0, 1), (2, 3), (4, 5), (6,), (7,))
+
+        def group_src(k, gi):
+            g = GROUPS[gi]
+            r = g[0] // 2
+            cols = slice(512 * (g[0] % 2), 512 * (g[-1] % 2 + 1))
+            if k == 2:
+                return nal[r][:, cols]
+            return ab[r][:, k].rearrange("p i n -> p (i n)")[:, cols]
+
+        def NEG(gi):
+            r = GROUPS[gi][0] // 2
+            if r not in nal:
+                nal[r] = sb.tile([P, 1024], BF16, name=f"nal{r}", align_bytes=64)
+            nc.vector.tensor_scalar(
+                out=group_src(2, gi), in0=group_src(0, gi), scalar1=-1.0, scalar2=None, op0=ALU.mult
+            )
+
+        def R(k, gi):
+            g = GROUPS[gi]
+            a, cols = g[0] // NT, slice(P * (g[0] % NT), P * (g[-1] % NT + 1))
+            nc.vector.quantize_mx(
+                out=kc[a][:, k, cols].bitcast(FP8X4), scales=ks[a][:, k, cols], in_=group_src(k, gi)
+            )
 
         def XX(a, n):
-            tag = "x" if a == 0 else ("t" if n < 2 else "ab")
-            x = px[a, n] = bank(tag, [P, N], f"px{a}_{n}")
+            x = px[a, n] = bank(4 + n if a == 0 else n, [P, N], f"px{a}_{n}")
             rows = slice(P * n, P * (n + 1))
             for s, m in ((0, 1), (1, 2)):
                 nc.tensor.matmul_mx(
@@ -227,49 +252,52 @@ def tile_generalpreferenceskewembeddingscores_d2p_kernel(
                     start=(s == 0),
                     stop=(s == 1),
                 )
+
+        def SIG(a, n):
             sig[a, n] = sb.tile([P, N], F32, name=f"sig{a}_{n}")
-            nc.scalar.activation(out=sig[a, n][:], in_=x[:], func=ACT.Sigmoid, scale=C)
+            nc.scalar.activation(out=sig[a, n][:], in_=px[a, n][:], func=ACT.Sigmoid, scale=C)
 
-        def LF(a, n):
+        def col_cuts(a, n):
+            last = (a, n) == (NP - 1, NT - 1)
+            return [slice(0, N // 2), slice(N // 2, N)] if last else [slice(0, N)]
+
+        def LOG(a, n):
             logs[a, n] = sb.tile([P, N], F32, name=f"logs{a}_{n}")
-            nc.scalar.activation(out=logs[a, n][:], in_=sig[a, n][:], func=ACT.Ln, bias=tiny[:])
-            o = sb.tile([P, N], F32, name=f"o{a}_{n}")
-            nc.vector.scalar_tensor_tensor(
-                out=o[:], in0=px[a, n][:], scalar=C, in1=logs[a, n][:], op0=ALU.mult, op1=ALU.min
-            )
-            nc.sync.dma_start(out=out[a, P * n : P * (n + 1), :], in_=o[:])
+            for cut in col_cuts(a, n):
+                nc.scalar.activation(
+                    out=logs[a, n][:, cut], in_=sig[a, n][:, cut], func=ACT.Ln, bias=tiny[:]
+                )
 
-        T_ALL = NP * NT
-        gate_turn()
-        for k in range(-4, T_ALL + 2):
-            if k == -4:
-                gate_ln()
-            if 0 <= k + 2 < T_ALL:
-                E(k + 2)
-            if k + 4 < T_ALL:
-                W(k + 4)
-            if k == -3:
-                PERM(0)
-            if k == -2:
-                PERM(1)
-            if k == -1:
-                gate_lam()
-            if k + 4 < T_ALL:
-                X(k + 4)
-            if 0 <= k + 2 < T_ALL:
-                Q(k + 2)
-            if 0 <= k < T_ALL:
-                A(k)
-                B(k)
-            for T in range(T_ALL):
-                if k == (T - 2 if T < 5 else T - 1):
-                    M(T)
-            if 1 <= k - 1 < T_ALL and (k - 1) % 2 == 1:
-                NR((k - 1) // 2)
-            for n in {6: (0,), 7: (1, 2, 3)}.get(k, ()):
-                XX(0, n)
-        for n in range(NT):
-            XX(1, n)
-        for a in range(NP):
-            for n in range(NT):
-                LF(a, n)
+        def FIN(a, n):
+            o = sb.tile([P, N], F32, name=f"o{a}_{n}")
+            for cut in col_cuts(a, n):
+                nc.vector.scalar_tensor_tensor(
+                    out=o[:, cut], in0=px[a, n][:, cut], scalar=C, in1=logs[a, n][:, cut],
+                    op0=ALU.mult, op1=ALU.min,
+                )
+                nc.sync.dma_start(out=out[a, P * n : P * (n + 1), cut], in_=o[:, cut])
+
+        ORDER = (
+            "gP W0 g1 W1 X0 W2 X1 E0 W3 E1 X2 Q0 g2 Pa X3 E2 Pb Ma0 W4 Mb0 Q1 W5 X4 g3 Mb1 lam Q2 E4 "
+            "A0 Ma1 E3 Q4 B0 Ma2 W6 Q3 X5 A2 Mb2 A1 Ma3 B2 W7 Ma4 E5 N0 X6 A4 Mb4 E6 Q5 X7 Rn0 B4 Q6 "
+            "Ma5 A3 E7 Mb5 B1 A5 Mb3 B5 N1 Ra2 Ma6 Rb0 B3 Q7 Mb6 Rn1 A6 B6 Ra0 Ma7 Rb1 Ra1 Rb2 XX00 "
+            "Rb3 N3 N2 Mb7 A7 S00 XX01 Ra3 Rn3 B7 N4 XX02 Rn2 S01 Ra4 Rn4 XX03 Rb4 S02 XX10 S03 XX11 "
+            "S10 XX12 S11 XX13 S12 S13 G00 G01 F00 G02 F01 G03 F02 G10 F03 G11 F10 G12 F11 G13 F12 "
+            "F13 "
+        )
+        steps = {"gP": gate_turn, "g1": gate_out, "g2": gate_exp, "g3": gate_ln, "lam": gate_lam}
+        kinds = {
+            "W": W, "X": X, "E": E, "Q": Q, "A": A, "B": B, "N": NEG,
+            "Ma": lambda T: M(0, T), "Mb": lambda T: M(1, T),
+            "Ra": lambda g: R(0, g), "Rb": lambda g: R(1, g), "Rn": lambda g: R(2, g),
+            "XX": lambda k: XX(k // 10, k % 10), "S": lambda k: SIG(k // 10, k % 10),
+            "G": lambda k: LOG(k // 10, k % 10), "F": lambda k: FIN(k // 10, k % 10),
+        }
+        for step in ORDER.split():
+            if step in steps:
+                steps[step]()
+            elif step in ("Pa", "Pb"):
+                PERM(0 if step == "Pa" else 1)
+            else:
+                head = "".join([ch for ch in step if ch not in "0123456789"])
+                kinds[head](int(step[len(head):]))

@@ -51,13 +51,13 @@ def tile_generalpreferenceskewembeddingscores_d2p_kernel(
         for w in range(2):
             nc.vector.memset(s_raw[w][:].rearrange("p g k -> p (g k)").bitcast(I32), 0)
         nc.vector.memset(tiny[:], TINY)
-        make_identity(nc, ident16[:])
-        make_identity(nc, ident[:])
 
-        nc.scalar.dma_start(
+        nc.gpsimd.dma_start(
             out=gate_rows[0:4, :].rearrange("t (q r) -> t q r", r=8),
             in_=gate.rearrange("a (q t r) -> t (a q) r", t=4, r=8),
         )
+        make_identity(nc, ident[:])
+        make_identity(nc, ident16[:])
         nc.scalar.dma_start(
             out=scales[:], in_=h_scale.rearrange("a i j -> (a i j)").partition_broadcast(P)
         )
@@ -87,14 +87,12 @@ def tile_generalpreferenceskewembeddingscores_d2p_kernel(
                 nc.sync.dma_start(out=d[32 * q : 32 * q + 4], in_=v[q])
 
         load_h(0, 0, 1)
-        load_h(0, 1, 1)
+        load_h(0, 1, 3)
         load_words(0, wa_words)
-        load_h(0, 2, 2)
         load_scales(0, wa_scales)
         load_words(1, wb_words)
         load_scales(1, wb_scales)
-        load_h(1, 0, 2)
-        load_h(1, 2, 2)
+        load_h(1, 0, 4)
 
         wide, pt, hg, hc, hs = {}, {}, {}, {}, {}
         pa, pb, ab, nal = {}, {}, {}, {}
@@ -167,15 +165,13 @@ def tile_generalpreferenceskewembeddingscores_d2p_kernel(
             nc.vector.quantize_mx(out=hc[T][:].bitcast(FP8X4), scales=hs[T][:], in_=hg[T][:])
 
         def PERM(w):
-            for g in range(G):
+            for dst, src, x in (
+                (w_perm[w][:].rearrange("p g t b -> p (g t b)"), w_raw[w][:].rearrange("p g b -> p (g b)"), 4),
+                (s_perm[w][:].rearrange("p g t b -> p (g t b)"), s_raw[w][:].rearrange("p g b -> p (g b)"), 2),
+            ):
                 nc.vector.tensor_copy(
-                    out=w_perm[w][:, g].rearrange("p t b -> p (t b)").bitcast(I32).rearrange("p (t q x) -> p q t x", t=4, x=4),
-                    in_=w_raw[w][:, g].bitcast(I32).rearrange("p (q t x) -> p q t x", t=4, x=4),
-                )
-            for g in range(G):
-                nc.vector.tensor_copy(
-                    out=s_perm[w][:, g].rearrange("p t b -> p (t b)").bitcast(I32).rearrange("p (t q x) -> p q t x", t=4, x=2),
-                    in_=s_raw[w][:, g].bitcast(I32).rearrange("p (q t x) -> p q t x", t=4, x=2),
+                    out=dst.bitcast(I32).rearrange("p (g t q x) -> p g q t x", g=G, t=4, x=x),
+                    in_=src.bitcast(I32).rearrange("p (g q t x) -> p g q t x", g=G, t=4, x=x),
                 )
 
         def M(w, T):
@@ -278,12 +274,11 @@ def tile_generalpreferenceskewembeddingscores_d2p_kernel(
                 nc.sync.dma_start(out=out[a, P * n : P * (n + 1), cut], in_=o[:, cut])
 
         ORDER = (
-            "gP W0 g1 W1 X0 W2 X1 E0 W3 E1 X2 Q0 g2 Pa X3 E2 Pb Ma0 W4 Mb0 Q1 W5 X4 g3 Mb1 lam Q2 E4 "
-            "A0 Ma1 E3 Q4 B0 Ma2 W6 Q3 X5 A2 Mb2 A1 Ma3 B2 W7 Ma4 E5 N0 X6 A4 Mb4 E6 Q5 X7 Rn0 B4 Q6 "
-            "Ma5 A3 E7 Mb5 B1 A5 Mb3 B5 N1 Ra2 Ma6 Rb0 B3 Q7 Mb6 Rn1 A6 B6 Ra0 Ma7 Rb1 Ra1 Rb2 XX00 "
-            "Rb3 N3 N2 Mb7 A7 S00 XX01 Ra3 Rn3 B7 N4 XX02 Rn2 S01 Ra4 Rn4 XX03 Rb4 S02 XX10 S03 XX11 "
-            "S10 XX12 S11 XX13 S12 S13 G00 G01 F00 G02 F01 G03 F02 G10 F03 G11 F10 G12 F11 G13 F12 "
-            "F13 "
+            "W0 W1 gP X0 W2 g1 X1 E0 W3 E1 Pa X2 g2 Q0 X3 Q1 Pb Ma0 W4 Mb1 g3 W5 E2 Mb0 E3 lam Q2 X4 "
+            "A0 B0 Ma1 W6 B1 X5 Q3 E4 Mb2 W7 Rb0 Ma2 Q4 B2 A1 X6 E5 Ma3 A2 Mb4 Q5 A3 Ma4 B4 N0 Mb3 N1 "
+            "E6 A4 Mb5 B3 Ra1 Q6 Ma5 Rn0 B5 Ra0 X7 A5 Mb6 E7 Rb1 Ma6 Rn1 B6 Ra2 Q7 XX00 A6 Mb7 N2 Ma7 "
+            "Rb3 Ra3 S00 N3 Rb2 XX01 Rn3 B7 A7 XX02 S01 Rn2 XX03 N4 S02 Ra4 Rb4 Rn4 S03 XX10 XX11 S10 "
+            "XX12 S11 XX13 S12 S13 G00 G01 F00 G02 F01 G03 F02 G10 F03 G11 F10 G12 F11 G13 F12 F13 "
         )
         steps = {"gP": gate_turn, "g1": gate_out, "g2": gate_exp, "g3": gate_ln, "lam": gate_lam}
         kinds = {

@@ -44,10 +44,8 @@ def tile_generalpreferenceskewembeddingscores_d2p_kernel(
         s_perm = [sb.tile([P, G, 4, P], U8, name=f"s_perm{w}", align_bytes=64) for w in range(2)]
         scales = sb.tile([P, NP * NT * 8], F32, name="scales")
         tiny = sb.tile([P, 1], F32, name="tiny")
-        warm = sb.tile([P, 1], F32, name="warm")
 
         nc.vector.memset(gate_rows[:], 0.0)
-        nc.vector.memset(warm[:], 0.0)
         for w in range(2):
             nc.vector.memset(s_raw[w][:].rearrange("p g k -> p (g k)").bitcast(I32), 0)
         nc.vector.memset(tiny[:], TINY)
@@ -61,7 +59,6 @@ def tile_generalpreferenceskewembeddingscores_d2p_kernel(
         nc.scalar.dma_start(
             out=scales[:], in_=h_scale.rearrange("a i j -> (a i j)").partition_broadcast(P)
         )
-        nc.scalar.activation(out=warm[:], in_=warm[:], func=ACT.Exp)
 
         codes_in = {}
 
@@ -176,7 +173,7 @@ def tile_generalpreferenceskewembeddingscores_d2p_kernel(
 
         def M(w, T):
             for store in ((pa, pb)[w],):
-                store[T] = bank({1: 4, 3: 6}.get(T, 2) + w, [P, 4, P], f"p{w}_{T}")
+                store[T] = bank((2, 4, 6, 2, 4, 6, 2, 2)[T] + w, [P, 4, P], f"p{w}_{T}")
                 for t in range(4):
                     for g in range(G):
                         nc.tensor.matmul_mx(
@@ -236,7 +233,7 @@ def tile_generalpreferenceskewembeddingscores_d2p_kernel(
             )
 
         def XX(a, n):
-            x = px[a, n] = bank(4 + n if a == 0 else n, [P, N], f"px{a}_{n}")
+            x = px[a, n] = bank((6, 7, 4, 5)[n] if a == 0 else n, [P, N], f"px{a}_{n}")
             rows = slice(P * n, P * (n + 1))
             for s, m in ((0, 1), (1, 2)):
                 nc.tensor.matmul_mx(
@@ -274,11 +271,12 @@ def tile_generalpreferenceskewembeddingscores_d2p_kernel(
                 nc.sync.dma_start(out=out[a, P * n : P * (n + 1), cut], in_=o[:, cut])
 
         ORDER = (
-            "W0 W1 gP X0 W2 g1 X1 E0 W3 E1 Pa X2 g2 Q0 X3 Q1 Pb Ma0 W4 Mb1 g3 W5 E2 Mb0 E3 lam Q2 X4 "
-            "A0 B0 Ma1 W6 B1 X5 Q3 E4 Mb2 W7 Rb0 Ma2 Q4 B2 A1 X6 E5 Ma3 A2 Mb4 Q5 A3 Ma4 B4 N0 Mb3 N1 "
-            "E6 A4 Mb5 B3 Ra1 Q6 Ma5 Rn0 B5 Ra0 X7 A5 Mb6 E7 Rb1 Ma6 Rn1 B6 Ra2 Q7 XX00 A6 Mb7 N2 Ma7 "
-            "Rb3 Ra3 S00 N3 Rb2 XX01 Rn3 B7 A7 XX02 S01 Rn2 XX03 N4 S02 Ra4 Rb4 Rn4 S03 XX10 XX11 S10 "
-            "XX12 S11 XX13 S12 S13 G00 G01 F00 G02 F01 G03 F02 G10 F03 G11 F10 G12 F11 G13 F12 F13 "
+            "W0 W1 X0 W2 E0 X1 W3 gP E1 X2 Pa g1 Q0 X3 W4 E2 Ma0 g2 Pb X4 Q2 Q1 Mb0 W5 Ma2 g3 W7 E3 "
+            "Ma1 E4 lam W6 X5 Q3 Mb1 A0 E5 X6 Q4 B1 A2 Ma3 B0 A1 Mb2 E6 Q5 X7 A3 B2 Ma5 N0 E7 Q6 Mb3 "
+            "Ra1 N1 Ma6 A5 B3 Mb5 Q7 Ra0 Mb4 A6 B5 Mb6 Rb0 B4 Rn0 Ma4 Ra3 N3 B6 Rb1 Ma7 Rn1 Rn3 Rb2 "
+            "XX00 A4 Mb7 A7 XX01 S00 Rb3 N2 N4 XX02 B7 Ra4 Ra2 XX03 Rn4 S01 Rn2 Rb4 S02 XX10 S03 XX11 "
+            "S10 XX12 S11 XX13 S12 S13 G00 G01 F00 G02 F01 G03 F02 G10 F03 G11 F10 G12 F11 G13 F12 "
+            "F13 "
         )
         steps = {"gP": gate_turn, "g1": gate_out, "g2": gate_exp, "g3": gate_ln, "lam": gate_lam}
         kinds = {

from contextlib import ExitStack

import concourse.mybir as mybir
from concourse.masks import make_identity

NP, N, D, K = 2, 512, 1024, 512
P = 128
NT = N // P
G = D // 512
FLOPS = 2 * NP * (2 * N * D * K + N * N * K)
C = K ** -0.5
TINY = 2.0 ** -60

F32 = mybir.dt.float32
BF16 = mybir.dt.bfloat16
I32 = mybir.dt.int32
U32 = mybir.dt.uint32
U8 = mybir.dt.uint8
FP8 = mybir.dt.float8_e4m3fn
FP8X4 = mybir.dt.float8_e4m3fn_x4
FP4X4 = mybir.dt.float4_e2m1fn_x4
ALU = mybir.AluOpType
ACT = mybir.ActivationFunctionType


def tile_generalpreferenceskewembeddingscores_d2p_kernel(
    tc, h_bytes, h_scale, wa_words, wa_scales, wb_words, wb_scales, gate, out
):
    nc = tc.nc
    with ExitStack() as ctx:
        sb = ctx.enter_context(tc.tile_pool(name="sb", bufs=1))
        ps = ctx.enter_context(tc.psum_pool(name="ps", bufs=1))
        ctx.enter_context(tc.manual_schedule())

        def bank(b, shape, name, dtype=F32):
            return ps.tile(shape, dtype, name=name, tag=f"bank{b}")

        gate_rows = sb.tile([P, NP * P], BF16, name="gate_rows")
        ident = sb.tile([P, P], F32, name="ident")
        ident16 = sb.tile([P, P], BF16, name="ident16")
        w_raw = [sb.tile([P, G, 1024], U8, name=f"w_raw{w}", align_bytes=64) for w in range(2)]
        w_perm = [sb.tile([P, G, 4, 256], U8, name=f"w_perm{w}", align_bytes=64) for w in range(2)]
        s_raw = [sb.tile([P, G, K], U8, name=f"s_raw{w}", align_bytes=64) for w in range(2)]
        s_perm = [sb.tile([P, G, 4, P], U8, name=f"s_perm{w}", align_bytes=64) for w in range(2)]
        scales = sb.tile([P, NP * NT * 8], F32, name="scales")
        tiny = sb.tile([P, 1], F32, name="tiny")

        nc.vector.memset(gate_rows[:], 0.0)
        for w in range(2):
            nc.vector.memset(s_raw[w][:].rearrange("p g k -> p (g k)").bitcast(I32), 0)
        nc.vector.memset(tiny[:], TINY)

        nc.gpsimd.dma_start(
            out=gate_rows[0:4, :].rearrange("t (q r) -> t q r", r=8),
            in_=gate.rearrange("a (q t r) -> t (a q) r", t=4, r=8),
        )
        make_identity(nc, ident[:])
        make_identity(nc, ident16[:])
        nc.scalar.dma_start(
            out=scales[:], in_=h_scale.rearrange("a i j -> (a i j)").partition_broadcast(P)
        )

        codes_in = {}

        def load_h(a, first, count):
            t = sb.tile([P, count, D], U8, name=f"h_bytes{a}_{first}", align_bytes=64)
            nc.sync.dma_start(
                out=t[:],
                in_=h_bytes[a, first * P : (first + count) * P, :].rearrange("(i p) k -> p i k", p=P),
            )
            for i in range(count):
                codes_in[a * NT + first + i] = (t, i)

        def load_words(w, words):
            nc.sync.dma_start(
                out=w_raw[w][:].rearrange("p g b -> p (g b)").bitcast(I32).rearrange("p (g c) -> p g c", g=G),
                in_=words.bitcast(I32).rearrange("g p c -> p g c"),
            )

        def load_scales(w, src):
            v = src.bitcast(I32).rearrange("g (q r) c -> q r g c", r=4)
            d = s_raw[w][:].rearrange("p g k -> p (g k)").bitcast(I32).rearrange("p (g c) -> p g c", g=G)
            for q in range(4):
                nc.sync.dma_start(out=d[32 * q : 32 * q + 4], in_=v[q])

        load_h(0, 0, 1)
        load_h(0, 1, 3)
        load_words(0, wa_words)
        load_scales(0, wa_scales)
        load_words(1, wb_words)
        load_scales(1, wb_scales)
        load_h(1, 0, 4)

        wide, pt, hg, hc, hs = {}, {}, {}, {}, {}
        pa, pb, ab, nal = {}, {}, {}, {}
        kc = [sb.tile([P, 3, N], U32, name=f"kc{a}", align_bytes=64) for a in range(NP)]
        ks = [sb.tile([P, 3, N], U8, name=f"ks{a}", align_bytes=64) for a in range(NP)]
        px, sig, logs = {}, {}, {}
        lam = sb.tile([P, NP, 4], F32, name="lam")
        g_sb = sb.tile([P, NP, 4], F32, name="g_sb")
        g_abs = sb.tile([P, NP, 4], F32, name="g_abs")
        g_exp = sb.tile([P, NP, 4], F32, name="g_exp")
        g_ln = sb.tile([P, NP, 4], F32, name="g_ln")

        ps_gate = {}

        def gate_turn():
            pg = bank(7, [P, NP, P], "pg", BF16)
            ps_gate["pg"] = pg
            for a in range(NP):
                nc.tensor.transpose(pg[:, a, :], gate_rows[:, P * a : P * (a + 1)], ident16[:])

        def gate_out():
            pg = ps_gate["pg"]
            nc.scalar.activation(out=g_abs[:], in_=pg[:, :, 0:4], func=ACT.Abs)
            nc.scalar.copy(out=g_sb[:], in_=pg[:, :, 0:4])

        def gate_exp():
            nc.scalar.activation(out=g_exp[:], in_=g_abs[:], func=ACT.Exp, scale=-1.0)

        def gate_ln():
            nc.scalar.activation(out=g_ln[:], in_=g_exp[:], func=ACT.Ln, bias=1.0)

        def gate_lam():
            nc.vector.scalar_tensor_tensor(
                out=lam[:], in0=g_sb[:], scalar=0.0, in1=g_ln[:], op0=ALU.max, op1=ALU.add
            )

        def W(T):
            t, i = codes_in[T]
            wide[T] = sb.tile([P, D], BF16, name=f"wide{T}", align_bytes=64)
            for j in range(8):
                nc.vector.tensor_scalar(
                    out=wide[T][:, 512 * (j // 4) : 512 * (j // 4 + 1)].rearrange("p (u w e) -> p w u e", u=2, e=2)[
                        :, 32 * (j % 4) : 32 * (j % 4 + 1)
                    ],
                    in0=t[:, i, P * j : P * (j + 1)].bitcast(FP8).rearrange("p (w u e) -> p w u e", u=2, e=2),
                    scalar1=scales[:, 8 * T + j : 8 * T + j + 1],
                    scalar2=None,
                    op0=ALU.mult,
                )

        def X(T):
            pt[T] = bank(T % 2, [P, 2 * G, P], f"pt{T}")
            words = wide[T][:].bitcast(F32)
            for g in range(G):
                for u in range(2):
                    nc.tensor.transpose(
                        pt[T][:, 2 * g + u, :], words[:, 256 * g + P * u : 256 * g + P * (u + 1)], ident[:]
                    )

        def E(T):
            hg[T] = sb.tile([P, G * P * 4], BF16, name=f"hg{T}", align_bytes=64)
            nc.scalar.copy(
                out=hg[T][:].bitcast(F32).rearrange("p (g n u) -> p g n u", g=G, u=2),
                in_=pt[T][:].rearrange("p (g u) n -> p g n u", g=G),
            )

        def Q(T):
            hc[T] = sb.tile([P, G * P], U32, name=f"hc{T}", align_bytes=64)
            hs[T] = sb.tile([P, G * P], U8, name=f"hs{T}", align_bytes=64)
            nc.vector.quantize_mx(out=hc[T][:].bitcast(FP8X4), scales=hs[T][:], in_=hg[T][:])

        def PERM(w):
            for dst, src, x in (
                (w_perm[w][:].rearrange("p g t b -> p (g t b)"), w_raw[w][:].rearrange("p g b -> p (g b)"), 4),
                (s_perm[w][:].rearrange("p g t b -> p (g t b)"), s_raw[w][:].rearrange("p g b -> p (g b)"), 2),
            ):
                nc.vector.tensor_copy(
                    out=dst.bitcast(I32).rearrange("p (g t q x) -> p g q t x", g=G, t=4, x=x),
                    in_=src.bitcast(I32).rearrange("p (g q t x) -> p g q t x", g=G, t=4, x=x),
                )

        def M(w, T):
            for store in ((pa, pb)[w],):
                store[T] = bank((2, 4, 6, 2, 4, 6, 2, 2)[T] + w, [P, 4, P], f"p{w}_{T}")
                for t in range(4):
                    for g in range(G):
                        nc.tensor.matmul_mx(
                            out=store[T][:, t, :],
                            lhsT=w_perm[w][:, g, t, :].bitcast(FP4X4),
                            lhsT_scale=s_perm[w][:, g, t, :],
                            rhs=hc[T][:, P * g : P * (g + 1)].bitcast(FP8X4),
                            rhs_scale=hs[T][:, P * g : P * (g + 1)],
                            start=(g == 0),
                            stop=(g == G - 1),
                        )

        def pair_tile(T):
            r = T // 2
            if r not in ab:
                ab[r] = sb.tile([P, 2, 2, 512], BF16, name=f"ab{r}", align_bytes=64)
            return ab[r]

        def A(T):
            a = T // NT
            nc.vector.tensor_tensor(
                out=pair_tile(T)[:, 0, T % 2, :].rearrange("p (n t) -> p n t", t=4),
                in0=pa[T][:].rearrange("p t n -> p n t"),
                in1=lam[:, a : a + 1, :].to_broadcast([P, P, 4]),
                op=ALU.mult,
            )

        def B(T):
            nc.scalar.copy(
                out=pair_tile(T)[:, 1, T % 2, :].rearrange("p (n t) -> p n t", t=4),
                in_=pb[T][:].rearrange("p t n -> p n t"),
            )

        GROUPS = ((0, 1), (2, 3), (4, 5), (6,), (7,))

        def group_src(k, gi):
            g = GROUPS[gi]
            r = g[0] // 2
            cols = slice(512 * (g[0] % 2), 512 * (g[-1] % 2 + 1))
            if k == 2:
                return nal[r][:, cols]
            return ab[r][:, k].rearrange("p i n -> p (i n)")[:, cols]

        def NEG(gi):
            r = GROUPS[gi][0] // 2
            if r not in nal:
                nal[r] = sb.tile([P, 1024], BF16, name=f"nal{r}", align_bytes=64)
            nc.vector.tensor_scalar(
                out=group_src(2, gi), in0=group_src(0, gi), scalar1=-1.0, scalar2=None, op0=ALU.mult
            )

        def R(k, gi):
            g = GROUPS[gi]
            a, cols = g[0] // NT, slice(P * (g[0] % NT), P * (g[-1] % NT + 1))
            nc.vector.quantize_mx(
                out=kc[a][:, k, cols].bitcast(FP8X4), scales=ks[a][:, k, cols], in_=group_src(k, gi)
            )

        def XX(a, n):
            x = px[a, n] = bank((6, 7, 4, 5)[n] if a == 0 else n, [P, N], f"px{a}_{n}")
            rows = slice(P * n, P * (n + 1))
            for s, m in ((0, 1), (1, 2)):
                nc.tensor.matmul_mx(
                    out=x[:],
                    lhsT=kc[a][:, s, rows].bitcast(FP8X4),
                    lhsT_scale=ks[a][:, s, rows],
                    rhs=kc[a][:, m, :].bitcast(FP8X4),
                    rhs_scale=ks[a][:, m, :],
                    start=(s == 0),
                    stop=(s == 1),
                )

        def SIG(a, n):
            sig[a, n] = sb.tile([P, N], F32, name=f"sig{a}_{n}")
            nc.scalar.activation(out=sig[a, n][:], in_=px[a, n][:], func=ACT.Sigmoid, scale=C)

        def col_cuts(a, n):
            last = (a, n) == (NP - 1, NT - 1)
            return [slice(0, N // 2), slice(N // 2, N)] if last else [slice(0, N)]

        def LOG(a, n):
            logs[a, n] = sb.tile([P, N], F32, name=f"logs{a}_{n}")
            for cut in col_cuts(a, n):
                nc.scalar.activation(
                    out=logs[a, n][:, cut], in_=sig[a, n][:, cut], func=ACT.Ln, bias=tiny[:]
                )

        def FIN(a, n):
            o = sb.tile([P, N], F32, name=f"o{a}_{n}")
            for cut in col_cuts(a, n):
                nc.vector.scalar_tensor_tensor(
                    out=o[:, cut], in0=px[a, n][:, cut], scalar=C, in1=logs[a, n][:, cut],
                    op0=ALU.mult, op1=ALU.min,
                )
                nc.sync.dma_start(out=out[a, P * n : P * (n + 1), cut], in_=o[:, cut])

        ORDER = (
            "W0 W1 X0 W2 E0 X1 W3 gP E1 X2 Pa g1 Q0 X3 W4 E2 Ma0 g2 Pb X4 Q2 Q1 Mb0 W5 Ma2 g3 W7 E3 "
            "Ma1 E4 lam W6 X5 Q3 Mb1 A0 E5 X6 Q4 B1 A2 Ma3 B0 A1 Mb2 E6 Q5 X7 A3 B2 Ma5 N0 E7 Q6 Mb3 "
            "Ra1 N1 Ma6 A5 B3 Mb5 Q7 Ra0 Mb4 A6 B5 Mb6 Rb0 B4 Rn0 Ma4 Ra3 N3 B6 Rb1 Ma7 Rn1 Rn3 Rb2 "
            "XX00 A4 Mb7 A7 XX01 S00 Rb3 N2 N4 XX02 B7 Ra4 Ra2 XX03 Rn4 S01 Rn2 Rb4 S02 XX10 S03 XX11 "
            "S10 XX12 S11 XX13 S12 S13 G00 G01 F00 G02 F01 G03 F02 G10 F03 G11 F10 G12 F11 G13 F12 "
            "F13 "
        )
        steps = {"gP": gate_turn, "g1": gate_out, "g2": gate_exp, "g3": gate_ln, "lam": gate_lam}
        kinds = {
            "W": W, "X": X, "E": E, "Q": Q, "A": A, "B": B, "N": NEG,
            "Ma": lambda T: M(0, T), "Mb": lambda T: M(1, T),
            "Ra": lambda g: R(0, g), "Rb": lambda g: R(1, g), "Rn": lambda g: R(2, g),
            "XX": lambda k: XX(k // 10, k % 10), "S": lambda k: SIG(k // 10, k % 10),
            "G": lambda k: LOG(k // 10, k % 10), "F": lambda k: FIN(k // 10, k % 10),
        }
        for step in ORDER.split():
            if step in steps:
                steps[step]()
            elif step in ("Pa", "Pb"):
                PERM(0 if step == "Pa" else 1)
            else:
                head = "".join([ch for ch in step if ch not in "0123456789"])
                kinds[head](int(step[len(head):]))
